import numpy as np
import ml_dtypes


def mxq(x, axis, fmt="e4m3"):
    dtype, down = {"e4m3": (ml_dtypes.float8_e4m3fn, 7), "e5m2": (ml_dtypes.float8_e5m2, 14)}[fmt]
    v = np.moveaxis(np.asarray(x, np.float32).astype(ml_dtypes.bfloat16).astype(np.float64), axis, -1)
    blocks = v.reshape(v.shape[:-1] + (-1, 32))
    amax = np.abs(blocks).max(-1, keepdims=True)
    byte = np.maximum(np.where(amax > 0, np.frexp(amax)[1] - 1 + 127, 0) - down, 1)
    scale = np.exp2(byte - 127.0)
    codes = (blocks / scale).astype(np.float32).astype(dtype).astype(np.float64)
    return np.moveaxis((codes * scale).reshape(v.shape), -1, axis)


WIDE = False


def mx_kscale(k):
    if not WIDE:
        return np.ones(k)
    levels = np.array([30, -30])
    if k % 512:
        return np.exp2(np.random.permutation(np.resize(levels, k // 32))).repeat(32)
    a = np.empty((k // 512, 16))
    for p in range(k // 512):
        a[p, :8] = np.random.permutation(np.resize(levels, 8))
        for g in range(8):
            far = levels[np.abs(levels - a[p, g]) >= 10]
            a[p, g + 8] = far[np.random.randint(len(far))]
    return np.exp2(a.ravel()).repeat(32)


def f64(x):
    return np.asarray(x).astype(np.float64)


def striped(idx):
    return np.tile(np.asarray(idx).reshape(-1, 16).T, (8, 1)).astype(np.uint16)


def unstriped(offs):
    return offs[:16].T.reshape(-1).astype(np.int64)


E2M1 = np.array([0.0, 0.5, 1.0, 1.5, 2.0, 3.0, 4.0, 6.0, -0.0, -0.5, -1.0, -1.5, -2.0, -3.0, -4.0, -6.0])


def pack_weight(w, fmt):
    k, n = w.shape
    w = f64(np.asarray(w, np.float32).astype(ml_dtypes.bfloat16)).reshape(k // 32, 32, n)
    amax = np.abs(w).max(1)
    if fmt == "e4m3":
        byte = np.frexp(amax)[1] - 1 + 127 - 7
    else:
        mant, ex = np.frexp(amax / 6.0)
        byte = np.where(mant > 0.5, ex, ex - 1) + 127
    byte = np.clip(np.where(amax > 0, byte, 1), 1, 254)
    scaled = (w * np.exp2(127.0 - byte)[:, None, :]).reshape(k, n).astype(np.float32)
    by_word = np.ascontiguousarray(scaled.reshape(k // 512, 128, 4, n).transpose(0, 1, 3, 2))
    if fmt == "e4m3":
        words = by_word.astype(ml_dtypes.float8_e4m3fn).view(np.uint8)
    else:
        c = by_word.astype(ml_dtypes.float4_e2m1fn).view(np.uint8) & 0xF
        words = (c[..., 0::2] | (c[..., 1::2] << 4)).reshape(k // 512, 128, 2 * n)
    return np.ascontiguousarray(words), np.ascontiguousarray(byte.astype(np.uint8).reshape(k // 512, 16, n))


def unpack_weight(words, scales, fmt):
    g, _, n = scales.shape
    words = np.ascontiguousarray(words).reshape(g, 128, n, -1)
    if fmt == "e4m3":
        vals = words.view(ml_dtypes.float8_e4m3fn).astype(np.float64)
    else:
        nib = np.empty((g, 128, n, 4), np.uint8)
        nib[..., 0::2] = words & 0xF
        nib[..., 1::2] = words >> 4
        vals = E2M1[nib]
    vals = vals * np.repeat(np.exp2(scales.astype(np.float64) - 127.0), 8, axis=1)[..., None]
    return vals.transpose(0, 1, 3, 2).reshape(g * 512, n)


K, T, J, R, F, Z, C, O, N, E = 512, 1024, 256, 512, 512, 1024, 512, 128, 256, 1024


def setup_inputs():
    n = np.random.standard_normal
    idx = np.random.permutation(T)[:J]
    idx2 = np.random.permutation(Z)[:J]
    idx3 = np.random.permutation(C)[:J]
    idx4 = np.random.permutation(C)[:O]
    idx5 = np.random.permutation(C)[:O]
    idx6 = np.random.permutation(J)[:O]
    idx7 = np.random.permutation(E)[:O]
    fk = mx_kscale(K)
    ff = mx_kscale(F)
    fr = mx_kscale(R)
    xtp = pack_weight(n((K, T)) / fk[:, None], "e2m1")
    xop = pack_weight(n((F, Z)) / ff[:, None], "e4m3")
    wp = pack_weight(n((K, R)) * 1 / np.sqrt(K) * fk[:, None] * fr, "e4m3")
    w2p = pack_weight(n((F, R)) * 1 / np.sqrt(F) * ff[:, None], "e2m1")
    wbp = pack_weight(n((R, N)) * 1 / np.sqrt(R) / fr[:, None], "e2m1")
    return {
        "xt_words": xtp[0],
        "xt_scales": xtp[1],
        "xo_words": xop[0],
        "xo_scales": xop[1],
        "w_words": wp[0],
        "w_scales": wp[1],
        "w2_words": w2p[0],
        "w2_scales": w2p[1],
        "wb_words": wbp[0],
        "wb_scales": wbp[1],
        "offs": striped(idx),
        "offs2": striped(idx2),
        "offs3": striped(idx3),
        "offs4": striped(idx4),
        "offs5": striped(idx5),
        "offs6": striped(idx6),
        "offs7": striped(idx7),
    }


def reference(xt_words, xt_scales, xo_words, xo_scales, w_words, w_scales, w2_words, w2_scales, wb_words, wb_scales, offs, offs2, offs3, offs4, offs5, offs6, offs7):
    idx = unstriped(offs)
    idx2 = unstriped(offs2)
    idx3 = unstriped(offs3)
    idx4 = unstriped(offs4)
    idx5 = unstriped(offs5)
    idx6 = unstriped(offs6)
    idx7 = unstriped(offs7)
    xtu = unpack_weight(xt_words, xt_scales, "e2m1")
    xou = unpack_weight(xo_words, xo_scales, "e4m3")
    wu = unpack_weight(w_words, w_scales, "e4m3")
    w2u = unpack_weight(w2_words, w2_scales, "e2m1")
    wbu = unpack_weight(wb_words, wb_scales, "e2m1")
    xtidxg = xtu[:, idx]
    a = wu.T @ xtidxg
    xoidx2g = xou[:, idx2]
    b = w2u.T @ xoidx2g
    lb = b[:, 0:1]
    lb2 = b[:, 128:129]
    la = a[:, 0:1]
    pw = np.zeros((R, C))
    pw[:, idx3] = a
    hid = np.maximum(pw[:, idx4] * lb, pw[:, idx5] * lb2) - b[:, idx6] * la
    hidq = mxq(hid, 0, "e5m2")
    p = wbu.T @ hidq
    y = np.zeros((N, E))
    y[:, idx7] = p
    return y

@@ -1,0 +1,182 @@
+from contextlib import ExitStack
+
+import concourse.mybir as mybir
+
+K, T, J, R, Z, C, O, N, E = 512, 1024, 256, 512, 1024, 512, 128, 256, 1024
+FLOPS = 2 * (K * R * J + K * R * J + R * N * O)
+
+F32 = mybir.dt.float32
+BF16 = mybir.dt.bfloat16
+I32 = mybir.dt.int32
+U32 = mybir.dt.uint32
+U16 = mybir.dt.uint16
+U8 = mybir.dt.uint8
+E4M3X4 = mybir.dt.float8_e4m3fn_x4
+E5M2X4 = mybir.dt.float8_e5m2_x4
+E2M1X4 = mybir.dt.float4_e2m1fn_x4
+COPY = mybir.ActivationFunctionType.Copy
+ALU = mybir.AluOpType
+
+P = 128
+PACK = 4
+QUADS = 4
+
+
+def tile_list_leadreads_twotab_one_scattered_kernel(
+    tc, xt_words, xt_scales, xo_words, xo_scales, w_words, w_scales, w2_words, w2_scales,
+    wb_words, wb_scales, offs, offs2, offs3, offs4, offs5, offs6, offs7, out,
+):
+    nc = tc.nc
+    with ExitStack() as ctx:
+        lists = ctx.enter_context(tc.tile_pool(name="lists", bufs=1))
+        sb = ctx.enter_context(tc.tile_pool(name="sb", bufs=1))
+        ps = ctx.enter_context(tc.psum_pool(name="ps", bufs=1))
+
+        def load_list(src, name):
+            tile = lists.tile(list(src.shape), U16, name=name)
+            nc.sync.dma_start(tile[:], src)
+            return tile
+
+        def zeroed_plane(width, name, tag):
+            plane = sb.tile([P, width], U8, name=name, tag=tag, align_bytes=64)
+            nc.vector.memset(plane[:].bitcast(I32), 0)
+            return plane
+
+        def load_plane(plane, src, quads):
+            for q in quads:
+                nc.sync.dma_start(plane[32 * q : 32 * q + 4, :].bitcast(I32), src[0, 4 * q : 4 * q + 4, :].bitcast(I32))
+
+        def load_plane_whole(plane, src, quads):
+            for q in quads:
+                rows = src[0, 4 * q : 4 * q + 4, :].bitcast(I32)
+                nc.sync.dma_start(plane[32 * q : 32 * q + 32, :].bitcast(I32), rows.unsqueeze(0).broadcast_to([8, 4, rows.shape[1]]))
+
+        def load_words(src, width, dtype, name, tag):
+            tile = sb.tile([P, width], dtype, name=name, tag=tag, align_bytes=64)
+            nc.sync.dma_start(tile[:].bitcast(I32), src.bitcast(I32))
+            return tile
+
+        xt_plane = sb.tile([P, T], U8, name="xt_plane", align_bytes=64)
+        w_plane = sb.tile([P, R], U8, name="w_plane", align_bytes=64)
+        xo_plane = zeroed_plane(Z, "xo_plane", "xo_plane")
+        w2_plane = zeroed_plane(R, "w2_plane", "w2_plane")
+        wb_plane = zeroed_plane(N, "wb_plane", "wb_plane")
+        board = [sb.tile([P, C], F32, name=f"board{t}") for t in range(PACK)]
+        for t in range(PACK):
+            nc.vector.memset(board[t][:], 0.0)
+
+        tokens = load_list(offs, "tokens")
+        load_plane_whole(xt_plane, xt_scales, range(QUADS))
+        load_plane_whole(w_plane, w_scales, range(1))
+        xt_w = load_words(xt_words[0], T, U16, "xt_w", "xt_w")
+        w_w = load_words(w_words[0].rearrange("p n t -> p (n t)"), R, U32, "w_w", "w_w")
+        load_plane_whole(w_plane, w_scales, range(1, QUADS))
+        w2_w = load_words(w2_words[0], R, U16, "w2_w", "a2")
+        xo_w = load_words(xo_words[0].rearrange("p n t -> p (n t)"), Z, U32, "xo_w", "xo_w")
+        notes = load_list(offs2, "notes")
+        board_put = load_list(offs3, "board_put")
+        load_plane(xo_plane, xo_scales, range(QUADS))
+        load_plane(w2_plane, w2_scales, range(QUADS))
+        slot_get = load_list(offs6, "slot_get")
+        board_get = load_list(offs4, "board_get")
+        board_get2 = load_list(offs5, "board_get2")
+        wb_w = load_words(wb_words[0], N, U16, "wb_w", "wb_w")
+        load_plane(wb_plane, wb_scales, range(QUADS))
+        page_put = load_list(offs7, "page_put")
+
+        def dealt(dst):
+            return dst[:].rearrange("p (t m) -> p m t", t=PACK)
+
+        def in_fours(src):
+            return src[:].rearrange("p (m t) -> p m t", t=PACK)
+
+        xt_gs = sb.tile([P, J], U8, name="xt_gs", align_bytes=64)
+        xt_gw = sb.tile([P, J], U16, name="xt_gw", align_bytes=64)
+        nc.vector.tensor_copy(xt_gs[:], xt_plane[:].indirect(tokens[:]))
+        nc.vector.tensor_copy(xt_gw[:], xt_w[:].indirect(tokens[:]))
+        w_dw = sb.tile([P, R], U32, name="w_dw", align_bytes=64)
+        w_ds = sb.tile([P, R], U8, name="w_ds", align_bytes=64)
+        nc.scalar.copy(dealt(w_dw), in_fours(w_w))
+        nc.vector.tensor_copy(dealt(w_ds), in_fours(w_plane))
+        a_ps = [ps.tile([P, J], F32, name=f"a_ps{t}", tag=f"bank{t}") for t in range(PACK)]
+        for t in range(PACK):
+            cols = slice(P * t, P * (t + 1))
+            nc.tensor.matmul_mx(out=a_ps[t][:], lhsT=w_dw[:, cols].bitcast(E4M3X4), lhsT_scale=w_ds[:, cols],
+                                rhs=xt_gw[:].bitcast(E2M1X4), rhs_scale=xt_gs[:], start=True, stop=True)
+
+        xo_gw = sb.tile([P, J], U32, name="xo_gw", tag="page1", align_bytes=64)
+        xo_gs = sb.tile([P, J], U8, name="xo_gs", align_bytes=64)
+        w2_dw = sb.tile([P, R], U16, name="w2_dw", tag="page0", align_bytes=64)
+        w2_ds = sb.tile([P, R], U8, name="w2_ds", tag="a3", align_bytes=64)
+        nc.vector.tensor_copy(xo_gw[:], xo_w[:].indirect(notes[:]))
+        nc.scalar.copy(dealt(w2_dw), in_fours(w2_w))
+        nc.vector.tensor_copy(xo_gs[:], xo_plane[:].indirect(notes[:]))
+        nc.vector.tensor_copy(dealt(w2_ds), in_fours(w2_plane))
+        b_ps = [ps.tile([P, J], F32, name=f"b_ps{t}", tag=f"bank{PACK + t}") for t in range(PACK)]
+        for t in range(PACK):
+            cols = slice(P * t, P * (t + 1))
+            nc.tensor.matmul_mx(out=b_ps[t][:], lhsT=w2_dw[:, cols].bitcast(E2M1X4), lhsT_scale=w2_ds[:, cols],
+                                rhs=xo_gw[:].bitcast(E4M3X4), rhs_scale=xo_gs[:], start=True, stop=True)
+
+        a = [sb.tile([P, J], F32, name=f"a{t}", tag=f"a{t}", align_bytes=64) for t in range(PACK)]
+        b = [sb.tile([P, J], F32, name=f"b{t}") for t in range(PACK)]
+        nc.scalar.activation(a[0][:], a_ps[0][:], COPY)
+        nc.scalar.activation(board[0][:].indirect(board_put[:]), a[0][:], COPY)
+        nc.vector.tensor_copy(a[1][:], a_ps[1][:])
+        nc.vector.tensor_copy(a[2][:], a_ps[2][:])
+        nc.vector.tensor_copy(board[1][:].indirect(board_put[:]), a[1][:])
+        nc.scalar.activation(board[2][:].indirect(board_put[:]), a[2][:], COPY)
+        for t in range(PACK):
+            nc.vector.tensor_copy(b[t][:], b_ps[t][:])
+        nc.vector.tensor_copy(a[3][:], a_ps[3][:])
+        nc.vector.tensor_copy(board[3][:].indirect(board_put[:]), a[3][:])
+
+        pages = [sb.tile([P, E], F32, name=f"page{u}", tag=f"page{u}", align_bytes=64) for u in range(2)]
+        for u in range(2):
+            nc.gpsimd.memset(pages[u][:], 0.0)
+
+        hid = sb.tile([P, O, PACK], BF16, name="hid", align_bytes=64)
+        taken = [sb.tile([P, 2, O], F32, name=f"taken{h}") for h in range(2)]
+        larger = [sb.tile([P, 2, O], F32, name=f"larger{h}") for h in range(2)]
+        first = [sb.tile([P, O], F32, name=f"first{t}") for t in range(PACK)]
+        second = [sb.tile([P, O], F32, name=f"second{t}") for t in range(PACK)]
+
+        def look_slots(t):
+            nc.scalar.activation(taken[t // 2][:, t % 2, :], b[t][:].indirect(slot_get[:]), COPY, scale=a[t][:, 0:1])
+
+        def look_board(t):
+            nc.scalar.activation(first[t][:], board[t][:].indirect(board_get[:]), COPY, scale=b[t][:, 0:1])
+            nc.scalar.activation(second[t][:], board[t][:].indirect(board_get2[:]), COPY, scale=b[t][:, 128:129])
+            nc.vector.tensor_tensor(larger[t // 2][:, t % 2, :], first[t][:], second[t][:], ALU.max)
+
+        def finish_pair(h):
+            nc.vector.tensor_tensor(hid[:, :, 2 * h : 2 * h + 2], larger[h][:].rearrange("p j o -> p o j"),
+                                    taken[h][:].rearrange("p j o -> p o j"), ALU.subtract)
+
+        look_board(0)
+        look_slots(0)
+        look_board(1)
+        look_slots(1)
+        finish_pair(0)
+        look_board(2)
+        look_slots(2)
+        look_slots(3)
+        look_board(3)
+        finish_pair(1)
+
+        hid_w = sb.tile([P, O], U32, name="hid_w", align_bytes=64)
+        hid_s = sb.tile([P, O], U8, name="hid_s", align_bytes=64)
+        nc.vector.quantize_mx(out=hid_w[:].bitcast(E5M2X4), scales=hid_s[:], in_=hid[:].rearrange("p o t -> p (o t)"))
+
+        p_ps = [ps.tile([P, O], F32, name=f"p_ps{u}", tag=f"bank{u}") for u in range(2)]
+        p = [sb.tile([P, O], F32, name=f"p{u}") for u in range(2)]
+        for u in range(2):
+            cols = slice(P * u, P * (u + 1))
+            nc.tensor.matmul_mx(out=p_ps[u][:], lhsT=wb_w[:, cols].bitcast(E2M1X4), lhsT_scale=wb_plane[:, cols],
+                                rhs=hid_w[:].bitcast(E5M2X4), rhs_scale=hid_s[:], start=True, stop=True)
+        nc.scalar.activation(p[0][:], p_ps[0][:], COPY)
+        nc.scalar.activation(pages[0][:].indirect(page_put[:]), p[0][:], COPY)
+        nc.scalar.dma_start(out[0:P, :], pages[0][:])
+        nc.vector.tensor_copy(p[1][:], p_ps[1][:])
+        nc.vector.tensor_copy(pages[1][:].indirect(page_put[:]), p[1][:])
+        nc.sync.dma_start(out[P : 2 * P, :], pages[1][:])

@@ -37,19 +37,19 @@ def tile_list_leadreads_twotab_one_scattered_kernel(
             nc.sync.dma_start(tile[:], src)
             return tile
 
-        def zeroed_plane(width, name, tag):
+        def zeroed_plane(engine, width, name, tag):
             plane = sb.tile([P, width], U8, name=name, tag=tag, align_bytes=64)
-            nc.vector.memset(plane[:].bitcast(I32), 0)
+            engine.memset(plane[:].bitcast(I32), 0)
             return plane
 
         def load_plane(plane, src, quads):
             for q in quads:
                 nc.sync.dma_start(plane[32 * q : 32 * q + 4, :].bitcast(I32), src[0, 4 * q : 4 * q + 4, :].bitcast(I32))
 
-        def load_plane_whole(plane, src, quads):
+        def load_plane_whole(queue, plane, src, quads):
             for q in quads:
                 rows = src[0, 4 * q : 4 * q + 4, :].bitcast(I32)
-                nc.sync.dma_start(plane[32 * q : 32 * q + 32, :].bitcast(I32), rows.unsqueeze(0).broadcast_to([8, 4, rows.shape[1]]))
+                queue.dma_start(plane[32 * q : 32 * q + 32, :].bitcast(I32), rows.unsqueeze(0).broadcast_to([8, 4, rows.shape[1]]))
 
         def load_words(src, width, dtype, name, tag):
             tile = sb.tile([P, width], dtype, name=name, tag=tag, align_bytes=64)
@@ -57,26 +57,39 @@ def tile_list_leadreads_twotab_one_scattered_kernel(
             return tile
 
         xt_plane = sb.tile([P, T], U8, name="xt_plane", align_bytes=64)
-        w_plane = sb.tile([P, R], U8, name="w_plane", align_bytes=64)
-        xo_plane = zeroed_plane(Z, "xo_plane", "xo_plane")
-        w2_plane = zeroed_plane(R, "w2_plane", "w2_plane")
-        wb_plane = zeroed_plane(N, "wb_plane", "wb_plane")
-        board = [sb.tile([P, C], F32, name=f"board{t}") for t in range(PACK)]
-        for t in range(PACK):
-            nc.vector.memset(board[t][:], 0.0)
+        w_plane = zeroed_plane(nc.vector, R, "w_plane", "w_plane")
+        w2_plane = zeroed_plane(nc.vector, R, "w2_plane", "w2_plane")
+        xo_plane = zeroed_plane(nc.vector, Z, "xo_plane", "xo_plane")
 
+        def zeroed_board(engine, t):
+            tile = sb.tile([P, C], F32, name=f"board{t}", tag=f"board{t}", align_bytes=64)
+            engine.memset(tile[:], 0.0)
+            return tile
+
+        board = [zeroed_board(nc.gpsimd, t) for t in range(2)]
+
+        wb_plane = zeroed_plane(nc.gpsimd, N, "wb_plane", "wb_plane")
+
+        def load_staged(src, name):
+            tile = sb.tile([PACK, QUADS, R], U8, name=name)
+            nc.sync.dma_start(tile[:].bitcast(I32), src[0].rearrange("(q r) n -> r q n", r=PACK).bitcast(I32))
+            return tile
+
+        def spread(plane, staged):
+            for q in range(QUADS):
+                nc.vector.tensor_copy(plane[32 * q : 32 * q + PACK, :].bitcast(I32), staged[:, q, :].bitcast(I32))
+
+        w_staged = load_staged(w_scales, "w_staged")
         tokens = load_list(offs, "tokens")
-        load_plane_whole(xt_plane, xt_scales, range(QUADS))
-        load_plane_whole(w_plane, w_scales, range(1))
+        load_plane_whole(nc.sync, xt_plane, xt_scales, range(QUADS))
         xt_w = load_words(xt_words[0], T, U16, "xt_w", "xt_w")
         w_w = load_words(w_words[0].rearrange("p n t -> p (n t)"), R, U32, "w_w", "w_w")
-        load_plane_whole(w_plane, w_scales, range(1, QUADS))
-        w2_w = load_words(w2_words[0], R, U16, "w2_w", "a2")
+        w2_w = load_words(w2_words[0], R, U16, "w2_w", "a0")
+        w2_staged = load_staged(w2_scales, "w2_staged")
         xo_w = load_words(xo_words[0].rearrange("p n t -> p (n t)"), Z, U32, "xo_w", "xo_w")
         notes = load_list(offs2, "notes")
-        board_put = load_list(offs3, "board_put")
         load_plane(xo_plane, xo_scales, range(QUADS))
-        load_plane(w2_plane, w2_scales, range(QUADS))
+        board_put = load_list(offs3, "board_put")
         slot_get = load_list(offs6, "slot_get")
         board_get = load_list(offs4, "board_get")
         board_get2 = load_list(offs5, "board_get2")
@@ -88,16 +101,17 @@ def tile_list_leadreads_twotab_one_scattered_kernel(
             return dst[:].rearrange("p (t m) -> p m t", t=PACK)
 
         def in_fours(src):
-            return src[:].rearrange("p (m t) -> p m t", t=PACK)
+            return src.rearrange("p (m t) -> p m t", t=PACK)
 
         xt_gs = sb.tile([P, J], U8, name="xt_gs", align_bytes=64)
         xt_gw = sb.tile([P, J], U16, name="xt_gw", align_bytes=64)
-        nc.vector.tensor_copy(xt_gs[:], xt_plane[:].indirect(tokens[:]))
-        nc.vector.tensor_copy(xt_gw[:], xt_w[:].indirect(tokens[:]))
         w_dw = sb.tile([P, R], U32, name="w_dw", align_bytes=64)
         w_ds = sb.tile([P, R], U8, name="w_ds", align_bytes=64)
-        nc.scalar.copy(dealt(w_dw), in_fours(w_w))
-        nc.vector.tensor_copy(dealt(w_ds), in_fours(w_plane))
+        spread(w_plane, w_staged)
+        nc.vector.tensor_copy(dealt(w_ds), in_fours(w_plane[:]))
+        nc.vector.tensor_copy(xt_gs[:], xt_plane[:].indirect(tokens[:]))
+        nc.vector.tensor_copy(xt_gw[:], xt_w[:].indirect(tokens[:]))
+        nc.scalar.copy(dealt(w_dw), in_fours(w_w[:]))
         a_ps = [ps.tile([P, J], F32, name=f"a_ps{t}", tag=f"bank{t}") for t in range(PACK)]
         for t in range(PACK):
             cols = slice(P * t, P * (t + 1))
@@ -105,13 +119,14 @@ def tile_list_leadreads_twotab_one_scattered_kernel(
                                 rhs=xt_gw[:].bitcast(E2M1X4), rhs_scale=xt_gs[:], start=True, stop=True)
 
         xo_gw = sb.tile([P, J], U32, name="xo_gw", tag="page1", align_bytes=64)
-        xo_gs = sb.tile([P, J], U8, name="xo_gs", align_bytes=64)
+        xo_gs = sb.tile([P, J], U8, name="xo_gs", tag="board2", align_bytes=64)
         w2_dw = sb.tile([P, R], U16, name="w2_dw", tag="page0", align_bytes=64)
-        w2_ds = sb.tile([P, R], U8, name="w2_ds", tag="a3", align_bytes=64)
+        w2_ds = sb.tile([P, R], U8, name="w2_ds", tag="board3", align_bytes=64)
+        nc.scalar.copy(dealt(w2_dw), in_fours(w2_w[:]))
+        spread(w2_plane, w2_staged)
+        nc.vector.tensor_copy(dealt(w2_ds), in_fours(w2_plane[:]))
         nc.vector.tensor_copy(xo_gw[:], xo_w[:].indirect(notes[:]))
-        nc.scalar.copy(dealt(w2_dw), in_fours(w2_w))
         nc.vector.tensor_copy(xo_gs[:], xo_plane[:].indirect(notes[:]))
-        nc.vector.tensor_copy(dealt(w2_ds), in_fours(w2_plane))
         b_ps = [ps.tile([P, J], F32, name=f"b_ps{t}", tag=f"bank{PACK + t}") for t in range(PACK)]
         for t in range(PACK):
             cols = slice(P * t, P * (t + 1))
@@ -120,16 +135,15 @@ def tile_list_leadreads_twotab_one_scattered_kernel(
 
         a = [sb.tile([P, J], F32, name=f"a{t}", tag=f"a{t}", align_bytes=64) for t in range(PACK)]
         b = [sb.tile([P, J], F32, name=f"b{t}") for t in range(PACK)]
-        nc.scalar.activation(a[0][:], a_ps[0][:], COPY)
-        nc.scalar.activation(board[0][:].indirect(board_put[:]), a[0][:], COPY)
-        nc.vector.tensor_copy(a[1][:], a_ps[1][:])
-        nc.vector.tensor_copy(a[2][:], a_ps[2][:])
-        nc.vector.tensor_copy(board[1][:].indirect(board_put[:]), a[1][:])
-        nc.scalar.activation(board[2][:].indirect(board_put[:]), a[2][:], COPY)
         for t in range(PACK):
+            nc.scalar.activation(a[t][:], a_ps[t][:], COPY)
+        nc.scalar.activation(board[0][:].indirect(board_put[:]), a[0][:], COPY)
+        nc.vector.tensor_copy(board[1][:].indirect(board_put[:]), a[1][:])
+        for t in range(2, PACK):
             nc.vector.tensor_copy(b[t][:], b_ps[t][:])
-        nc.vector.tensor_copy(a[3][:], a_ps[3][:])
-        nc.vector.tensor_copy(board[3][:].indirect(board_put[:]), a[3][:])
+        for t in range(2, PACK):
+            board.append(zeroed_board(nc.gpsimd, t))
+            nc.vector.tensor_copy(board[t][:].indirect(board_put[:]), a[t][:])
 
         pages = [sb.tile([P, E], F32, name=f"page{u}", tag=f"page{u}", align_bytes=64) for u in range(2)]
         for u in range(2):
@@ -137,7 +151,7 @@ def tile_list_leadreads_twotab_one_scattered_kernel(
 
         hid = sb.tile([P, O, PACK], BF16, name="hid", align_bytes=64)
         taken = [sb.tile([P, 2, O], F32, name=f"taken{h}") for h in range(2)]
-        larger = [sb.tile([P, 2, O], F32, name=f"larger{h}") for h in range(2)]
+        larger = sb.tile([P, PACK, O], F32, name="larger", tag="a3", align_bytes=64)
         first = [sb.tile([P, O], F32, name=f"first{t}") for t in range(PACK)]
         second = [sb.tile([P, O], F32, name=f"second{t}") for t in range(PACK)]
 
@@ -147,22 +161,26 @@ def tile_list_leadreads_twotab_one_scattered_kernel(
         def look_board(t):
             nc.scalar.activation(first[t][:], board[t][:].indirect(board_get[:]), COPY, scale=b[t][:, 0:1])
             nc.scalar.activation(second[t][:], board[t][:].indirect(board_get2[:]), COPY, scale=b[t][:, 128:129])
-            nc.vector.tensor_tensor(larger[t // 2][:, t % 2, :], first[t][:], second[t][:], ALU.max)
+
+        def keep_larger(t):
+            nc.vector.tensor_tensor(larger[:, t, :], first[t][:], second[t][:], ALU.max)
 
         def finish_pair(h):
-            nc.vector.tensor_tensor(hid[:, :, 2 * h : 2 * h + 2], larger[h][:].rearrange("p j o -> p o j"),
+            nc.vector.tensor_tensor(hid[:, :, 2 * h : 2 * h + 2], larger[:, 2 * h : 2 * h + 2, :].rearrange("p j o -> p o j"),
                                     taken[h][:].rearrange("p j o -> p o j"), ALU.subtract)
 
-        look_board(0)
-        look_slots(0)
-        look_board(1)
-        look_slots(1)
-        finish_pair(0)
-        look_board(2)
-        look_slots(2)
-        look_slots(3)
-        look_board(3)
-        finish_pair(1)
+        for t in range(2):
+            nc.scalar.activation(b[t][:], b_ps[t][:], COPY)
+            look_board(t)
+            look_slots(t)
+        for t in range(2, PACK):
+            look_slots(t)
+        for t in range(2, PACK):
+            look_board(t)
+        for h in range(2):
+            keep_larger(2 * h)
+            keep_larger(2 * h + 1)
+            finish_pair(h)
 
         hid_w = sb.tile([P, O], U32, name="hid_w", align_bytes=64)
         hid_s = sb.tile([P, O], U8, name="hid_s", align_bytes=64)

@@ -42,9 +42,9 @@ def tile_list_leadreads_twotab_one_scattered_kernel(
             engine.memset(plane[:].bitcast(I32), 0)
             return plane
 
-        def load_plane(plane, src, quads):
+        def load_plane(queue, plane, src, quads):
             for q in quads:
-                nc.sync.dma_start(plane[32 * q : 32 * q + 4, :].bitcast(I32), src[0, 4 * q : 4 * q + 4, :].bitcast(I32))
+                queue.dma_start(plane[32 * q : 32 * q + 4, :].bitcast(I32), src[0, 4 * q : 4 * q + 4, :].bitcast(I32))
 
         def load_plane_whole(queue, plane, src, quads):
             for q in quads:
@@ -56,45 +56,38 @@ def tile_list_leadreads_twotab_one_scattered_kernel(
             nc.sync.dma_start(tile[:].bitcast(I32), src.bitcast(I32))
             return tile
 
-        xt_plane = sb.tile([P, T], U8, name="xt_plane", align_bytes=64)
-        w_plane = zeroed_plane(nc.vector, R, "w_plane", "w_plane")
-        w2_plane = zeroed_plane(nc.vector, R, "w2_plane", "w2_plane")
+        xt_plane = sb.tile([P, T], U8, name="xt_plane", tag="board3", align_bytes=64)
         xo_plane = zeroed_plane(nc.vector, Z, "xo_plane", "xo_plane")
+        load_plane(nc.gpsimd, xo_plane, xo_scales, range(2, QUADS))
+        ww_plane = zeroed_plane(nc.vector, 2 * R, "ww_plane", "ww_plane")
 
         def zeroed_board(engine, t):
             tile = sb.tile([P, C], F32, name=f"board{t}", tag=f"board{t}", align_bytes=64)
             engine.memset(tile[:], 0.0)
             return tile
 
-        board = [zeroed_board(nc.gpsimd, t) for t in range(2)]
+        board = [zeroed_board(nc.vector, t) for t in range(2)]
 
-        wb_plane = zeroed_plane(nc.gpsimd, N, "wb_plane", "wb_plane")
+        wb_plane = zeroed_plane(nc.vector, N, "wb_plane", "wb_plane")
 
-        def load_staged(src, name):
-            tile = sb.tile([PACK, QUADS, R], U8, name=name)
-            nc.sync.dma_start(tile[:].bitcast(I32), src[0].rearrange("(q r) n -> r q n", r=PACK).bitcast(I32))
-            return tile
-
-        def spread(plane, staged):
-            for q in range(QUADS):
-                nc.vector.tensor_copy(plane[32 * q : 32 * q + PACK, :].bitcast(I32), staged[:, q, :].bitcast(I32))
-
-        w_staged = load_staged(w_scales, "w_staged")
+        staged = sb.tile([PACK, QUADS, 2 * R], U8, name="staged")
+        for i, src in enumerate((w_scales, w2_scales)):
+            nc.sync.dma_start(staged[:, :, R * i : R * (i + 1)].bitcast(I32), src[0].rearrange("(q r) n -> r q n", r=PACK).bitcast(I32))
         tokens = load_list(offs, "tokens")
-        load_plane_whole(nc.sync, xt_plane, xt_scales, range(QUADS))
+        load_plane_whole(nc.sync, xt_plane, xt_scales, range(QUADS - 1))
         xt_w = load_words(xt_words[0], T, U16, "xt_w", "xt_w")
         w_w = load_words(w_words[0].rearrange("p n t -> p (n t)"), R, U32, "w_w", "w_w")
+        load_plane_whole(nc.sync, xt_plane, xt_scales, range(QUADS - 1, QUADS))
         w2_w = load_words(w2_words[0], R, U16, "w2_w", "a0")
-        w2_staged = load_staged(w2_scales, "w2_staged")
         xo_w = load_words(xo_words[0].rearrange("p n t -> p (n t)"), Z, U32, "xo_w", "xo_w")
         notes = load_list(offs2, "notes")
-        load_plane(xo_plane, xo_scales, range(QUADS))
+        load_plane(nc.sync, xo_plane, xo_scales, range(2))
         board_put = load_list(offs3, "board_put")
         slot_get = load_list(offs6, "slot_get")
         board_get = load_list(offs4, "board_get")
         board_get2 = load_list(offs5, "board_get2")
         wb_w = load_words(wb_words[0], N, U16, "wb_w", "wb_w")
-        load_plane(wb_plane, wb_scales, range(QUADS))
+        load_plane(nc.sync, wb_plane, wb_scales, range(QUADS))
         page_put = load_list(offs7, "page_put")
 
         def dealt(dst):
@@ -107,10 +100,11 @@ def tile_list_leadreads_twotab_one_scattered_kernel(
         xt_gw = sb.tile([P, J], U16, name="xt_gw", align_bytes=64)
         w_dw = sb.tile([P, R], U32, name="w_dw", align_bytes=64)
         w_ds = sb.tile([P, R], U8, name="w_ds", align_bytes=64)
-        spread(w_plane, w_staged)
-        nc.vector.tensor_copy(dealt(w_ds), in_fours(w_plane[:]))
-        nc.vector.tensor_copy(xt_gs[:], xt_plane[:].indirect(tokens[:]))
+        for q in range(QUADS):
+            nc.vector.tensor_copy(ww_plane[32 * q : 32 * q + PACK, :].bitcast(I32), staged[:, q, :].bitcast(I32))
+        nc.vector.tensor_copy(dealt(w_ds), in_fours(ww_plane[:, 0:R]))
         nc.vector.tensor_copy(xt_gw[:], xt_w[:].indirect(tokens[:]))
+        nc.vector.tensor_copy(xt_gs[:], xt_plane[:].indirect(tokens[:]))
         nc.scalar.copy(dealt(w_dw), in_fours(w_w[:]))
         a_ps = [ps.tile([P, J], F32, name=f"a_ps{t}", tag=f"bank{t}") for t in range(PACK)]
         for t in range(PACK):
@@ -123,8 +117,7 @@ def tile_list_leadreads_twotab_one_scattered_kernel(
         w2_dw = sb.tile([P, R], U16, name="w2_dw", tag="page0", align_bytes=64)
         w2_ds = sb.tile([P, R], U8, name="w2_ds", tag="board3", align_bytes=64)
         nc.scalar.copy(dealt(w2_dw), in_fours(w2_w[:]))
-        spread(w2_plane, w2_staged)
-        nc.vector.tensor_copy(dealt(w2_ds), in_fours(w2_plane[:]))
+        nc.vector.tensor_copy(dealt(w2_ds), in_fours(ww_plane[:, R : 2 * R]))
         nc.vector.tensor_copy(xo_gw[:], xo_w[:].indirect(notes[:]))
         nc.vector.tensor_copy(xo_gs[:], xo_plane[:].indirect(notes[:]))
         b_ps = [ps.tile([P, J], F32, name=f"b_ps{t}", tag=f"bank{PACK + t}") for t in range(PACK)]
@@ -139,8 +132,7 @@ def tile_list_leadreads_twotab_one_scattered_kernel(
             nc.scalar.activation(a[t][:], a_ps[t][:], COPY)
         nc.scalar.activation(board[0][:].indirect(board_put[:]), a[0][:], COPY)
         nc.vector.tensor_copy(board[1][:].indirect(board_put[:]), a[1][:])
-        for t in range(2, PACK):
-            nc.vector.tensor_copy(b[t][:], b_ps[t][:])
+        nc.vector.tensor_copy(b[3][:], b_ps[3][:])
         for t in range(2, PACK):
             board.append(zeroed_board(nc.gpsimd, t))
             nc.vector.tensor_copy(board[t][:].indirect(board_put[:]), a[t][:])
@@ -173,6 +165,7 @@ def tile_list_leadreads_twotab_one_scattered_kernel(
             nc.scalar.activation(b[t][:], b_ps[t][:], COPY)
             look_board(t)
             look_slots(t)
+        nc.scalar.activation(b[2][:], b_ps[2][:], COPY)
         for t in range(2, PACK):
             look_slots(t)
         for t in range(2, PACK):

from contextlib import ExitStack

import concourse.mybir as mybir

K, T, J, R, Z, C, O, N, E = 512, 1024, 256, 512, 1024, 512, 128, 256, 1024
FLOPS = 2 * (K * R * J + K * R * J + R * N * O)

F32 = mybir.dt.float32
BF16 = mybir.dt.bfloat16
I32 = mybir.dt.int32
U32 = mybir.dt.uint32
U16 = mybir.dt.uint16
U8 = mybir.dt.uint8
E4M3X4 = mybir.dt.float8_e4m3fn_x4
E5M2X4 = mybir.dt.float8_e5m2_x4
E2M1X4 = mybir.dt.float4_e2m1fn_x4
COPY = mybir.ActivationFunctionType.Copy
ALU = mybir.AluOpType

P = 128
PACK = 4
QUADS = 4


def tile_list_leadreads_twotab_one_scattered_kernel(
    tc, xt_words, xt_scales, xo_words, xo_scales, w_words, w_scales, w2_words, w2_scales,
    wb_words, wb_scales, offs, offs2, offs3, offs4, offs5, offs6, offs7, out,
):
    nc = tc.nc
    with ExitStack() as ctx:
        lists = ctx.enter_context(tc.tile_pool(name="lists", bufs=1))
        sb = ctx.enter_context(tc.tile_pool(name="sb", bufs=1))
        ps = ctx.enter_context(tc.psum_pool(name="ps", bufs=1))

        def load_list(src, name):
            tile = lists.tile(list(src.shape), U16, name=name)
            nc.sync.dma_start(tile[:], src)
            return tile

        def zeroed_plane(engine, width, name, tag):
            plane = sb.tile([P, width], U8, name=name, tag=tag, align_bytes=64)
            engine.memset(plane[:].bitcast(I32), 0)
            return plane

        def load_plane(queue, plane, src, quads):
            for q in quads:
                queue.dma_start(plane[32 * q : 32 * q + 4, :].bitcast(I32), src[0, 4 * q : 4 * q + 4, :].bitcast(I32))

        def load_plane_whole(queue, plane, src, quads):
            for q in quads:
                rows = src[0, 4 * q : 4 * q + 4, :].bitcast(I32)
                queue.dma_start(plane[32 * q : 32 * q + 32, :].bitcast(I32), rows.unsqueeze(0).broadcast_to([8, 4, rows.shape[1]]))

        def load_words(src, width, dtype, name, tag):
            tile = sb.tile([P, width], dtype, name=name, tag=tag, align_bytes=64)
            nc.sync.dma_start(tile[:].bitcast(I32), src.bitcast(I32))
            return tile

        xt_plane = sb.tile([P, T], U8, name="xt_plane", tag="board3", align_bytes=64)
        xo_plane = zeroed_plane(nc.vector, Z, "xo_plane", "xo_plane")
        load_plane(nc.gpsimd, xo_plane, xo_scales, range(2, QUADS))
        ww_plane = zeroed_plane(nc.vector, 2 * R, "ww_plane", "ww_plane")

        def zeroed_board(engine, t):
            tile = sb.tile([P, C], F32, name=f"board{t}", tag=f"board{t}", align_bytes=64)
            engine.memset(tile[:], 0.0)
            return tile

        board = [zeroed_board(nc.vector, t) for t in range(2)]

        wb_plane = zeroed_plane(nc.vector, N, "wb_plane", "wb_plane")

        staged = sb.tile([PACK, QUADS, 2 * R], U8, name="staged")
        for i, src in enumerate((w_scales, w2_scales)):
            nc.sync.dma_start(staged[:, :, R * i : R * (i + 1)].bitcast(I32), src[0].rearrange("(q r) n -> r q n", r=PACK).bitcast(I32))
        tokens = load_list(offs, "tokens")
        load_plane_whole(nc.sync, xt_plane, xt_scales, range(QUADS - 1))
        xt_w = load_words(xt_words[0], T, U16, "xt_w", "xt_w")
        w_w = load_words(w_words[0].rearrange("p n t -> p (n t)"), R, U32, "w_w", "w_w")
        load_plane_whole(nc.sync, xt_plane, xt_scales, range(QUADS - 1, QUADS))
        w2_w = load_words(w2_words[0], R, U16, "w2_w", "a0")
        xo_w = load_words(xo_words[0].rearrange("p n t -> p (n t)"), Z, U32, "xo_w", "xo_w")
        notes = load_list(offs2, "notes")
        load_plane(nc.sync, xo_plane, xo_scales, range(2))
        board_put = load_list(offs3, "board_put")
        slot_get = load_list(offs6, "slot_get")
        board_get = load_list(offs4, "board_get")
        board_get2 = load_list(offs5, "board_get2")
        wb_w = load_words(wb_words[0], N, U16, "wb_w", "wb_w")
        load_plane(nc.sync, wb_plane, wb_scales, range(QUADS))
        page_put = load_list(offs7, "page_put")

        def dealt(dst):
            return dst[:].rearrange("p (t m) -> p m t", t=PACK)

        def in_fours(src):
            return src.rearrange("p (m t) -> p m t", t=PACK)

        xt_gs = sb.tile([P, J], U8, name="xt_gs", align_bytes=64)
        xt_gw = sb.tile([P, J], U16, name="xt_gw", align_bytes=64)
        w_dw = sb.tile([P, R], U32, name="w_dw", align_bytes=64)
        w_ds = sb.tile([P, R], U8, name="w_ds", align_bytes=64)
        for q in range(QUADS):
            nc.vector.tensor_copy(ww_plane[32 * q : 32 * q + PACK, :].bitcast(I32), staged[:, q, :].bitcast(I32))
        nc.vector.tensor_copy(dealt(w_ds), in_fours(ww_plane[:, 0:R]))
        nc.vector.tensor_copy(xt_gw[:], xt_w[:].indirect(tokens[:]))
        nc.vector.tensor_copy(xt_gs[:], xt_plane[:].indirect(tokens[:]))
        nc.scalar.copy(dealt(w_dw), in_fours(w_w[:]))
        a_ps = [ps.tile([P, J], F32, name=f"a_ps{t}", tag=f"bank{t}") for t in range(PACK)]
        for t in range(PACK):
            cols = slice(P * t, P * (t + 1))
            nc.tensor.matmul_mx(out=a_ps[t][:], lhsT=w_dw[:, cols].bitcast(E4M3X4), lhsT_scale=w_ds[:, cols],
                                rhs=xt_gw[:].bitcast(E2M1X4), rhs_scale=xt_gs[:], start=True, stop=True)

        xo_gw = sb.tile([P, J], U32, name="xo_gw", tag="page1", align_bytes=64)
        xo_gs = sb.tile([P, J], U8, name="xo_gs", tag="board2", align_bytes=64)
        w2_dw = sb.tile([P, R], U16, name="w2_dw", tag="page0", align_bytes=64)
        w2_ds = sb.tile([P, R], U8, name="w2_ds", tag="board3", align_bytes=64)
        nc.scalar.copy(dealt(w2_dw), in_fours(w2_w[:]))
        nc.vector.tensor_copy(dealt(w2_ds), in_fours(ww_plane[:, R : 2 * R]))
        nc.vector.tensor_copy(xo_gw[:], xo_w[:].indirect(notes[:]))
        nc.vector.tensor_copy(xo_gs[:], xo_plane[:].indirect(notes[:]))
        b_ps = [ps.tile([P, J], F32, name=f"b_ps{t}", tag=f"bank{PACK + t}") for t in range(PACK)]
        for t in range(PACK):
            cols = slice(P * t, P * (t + 1))
            nc.tensor.matmul_mx(out=b_ps[t][:], lhsT=w2_dw[:, cols].bitcast(E2M1X4), lhsT_scale=w2_ds[:, cols],
                                rhs=xo_gw[:].bitcast(E4M3X4), rhs_scale=xo_gs[:], start=True, stop=True)

        a = [sb.tile([P, J], F32, name=f"a{t}", tag=f"a{t}", align_bytes=64) for t in range(PACK)]
        b = [sb.tile([P, J], F32, name=f"b{t}") for t in range(PACK)]
        for t in range(PACK):
            nc.scalar.activation(a[t][:], a_ps[t][:], COPY)
        nc.scalar.activation(board[0][:].indirect(board_put[:]), a[0][:], COPY)
        nc.vector.tensor_copy(board[1][:].indirect(board_put[:]), a[1][:])
        nc.vector.tensor_copy(b[3][:], b_ps[3][:])
        for t in range(2, PACK):
            board.append(zeroed_board(nc.gpsimd, t))
            nc.vector.tensor_copy(board[t][:].indirect(board_put[:]), a[t][:])

        pages = [sb.tile([P, E], F32, name=f"page{u}", tag=f"page{u}", align_bytes=64) for u in range(2)]
        for u in range(2):
            nc.gpsimd.memset(pages[u][:], 0.0)

        hid = sb.tile([P, O, PACK], BF16, name="hid", align_bytes=64)
        taken = [sb.tile([P, 2, O], F32, name=f"taken{h}") for h in range(2)]
        larger = sb.tile([P, PACK, O], F32, name="larger", tag="a3", align_bytes=64)
        first = [sb.tile([P, O], F32, name=f"first{t}") for t in range(PACK)]
        second = [sb.tile([P, O], F32, name=f"second{t}") for t in range(PACK)]

        def look_slots(t):
            nc.scalar.activation(taken[t // 2][:, t % 2, :], b[t][:].indirect(slot_get[:]), COPY, scale=a[t][:, 0:1])

        def look_board(t):
            nc.scalar.activation(first[t][:], board[t][:].indirect(board_get[:]), COPY, scale=b[t][:, 0:1])
            nc.scalar.activation(second[t][:], board[t][:].indirect(board_get2[:]), COPY, scale=b[t][:, 128:129])

        def keep_larger(t):
            nc.vector.tensor_tensor(larger[:, t, :], first[t][:], second[t][:], ALU.max)

        def finish_pair(h):
            nc.vector.tensor_tensor(hid[:, :, 2 * h : 2 * h + 2], larger[:, 2 * h : 2 * h + 2, :].rearrange("p j o -> p o j"),
                                    taken[h][:].rearrange("p j o -> p o j"), ALU.subtract)

        for t in range(2):
            nc.scalar.activation(b[t][:], b_ps[t][:], COPY)
            look_board(t)
            look_slots(t)
        nc.scalar.activation(b[2][:], b_ps[2][:], COPY)
        for t in range(2, PACK):
            look_slots(t)
        for t in range(2, PACK):
            look_board(t)
        for h in range(2):
            keep_larger(2 * h)
            keep_larger(2 * h + 1)
            finish_pair(h)

        hid_w = sb.tile([P, O], U32, name="hid_w", align_bytes=64)
        hid_s = sb.tile([P, O], U8, name="hid_s", align_bytes=64)
        nc.vector.quantize_mx(out=hid_w[:].bitcast(E5M2X4), scales=hid_s[:], in_=hid[:].rearrange("p o t -> p (o t)"))

        p_ps = [ps.tile([P, O], F32, name=f"p_ps{u}", tag=f"bank{u}") for u in range(2)]
        p = [sb.tile([P, O], F32, name=f"p{u}") for u in range(2)]
        for u in range(2):
            cols = slice(P * u, P * (u + 1))
            nc.tensor.matmul_mx(out=p_ps[u][:], lhsT=wb_w[:, cols].bitcast(E2M1X4), lhsT_scale=wb_plane[:, cols],
                                rhs=hid_w[:].bitcast(E5M2X4), rhs_scale=hid_s[:], start=True, stop=True)
        nc.scalar.activation(p[0][:], p_ps[0][:], COPY)
        nc.scalar.activation(pages[0][:].indirect(page_put[:]), p[0][:], COPY)
        nc.scalar.dma_start(out[0:P, :], pages[0][:])
        nc.vector.tensor_copy(p[1][:], p_ps[1][:])
        nc.vector.tensor_copy(pages[1][:].indirect(page_put[:]), p[1][:])
        nc.sync.dma_start(out[P : 2 * P, :], pages[1][:])
